import numpy as np
import ml_dtypes


def mxq(x, axis, fmt="e4m3"):
    dtype, down = {"e4m3": (ml_dtypes.float8_e4m3fn, 7), "e5m2": (ml_dtypes.float8_e5m2, 14)}[fmt]
    v = np.moveaxis(np.asarray(x, np.float32).astype(ml_dtypes.bfloat16).astype(np.float64), axis, -1)
    blocks = v.reshape(v.shape[:-1] + (-1, 32))
    amax = np.abs(blocks).max(-1, keepdims=True)
    byte = np.maximum(np.where(amax > 0, np.frexp(amax)[1] - 1 + 127, 0) - down, 1)
    scale = np.exp2(byte - 127.0)
    codes = (blocks / scale).astype(np.float32).astype(dtype).astype(np.float64)
    return np.moveaxis((codes * scale).reshape(v.shape), -1, axis)


WIDE = False


def mx_kscale(k):
    if not WIDE:
        return np.ones(k)
    levels = np.array([10, -10, 5, -5, 0])
    if k % 512:
        return np.exp2(np.random.permutation(np.resize(levels, k // 32))).repeat(32)
    a = np.empty((k // 512, 16))
    for p in range(k // 512):
        a[p, :8] = np.random.permutation(np.resize(levels, 8))
        for g in range(8):
            far = levels[np.abs(levels - a[p, g]) >= 10]
            a[p, g + 8] = far[np.random.randint(len(far))]
    return np.exp2(a.ravel()).repeat(32)


def f64(x):
    return np.asarray(x).astype(np.float64)


def striped(idx):
    return np.tile(idx.reshape(-1, 16).T, (8, 1)).astype(np.uint16)


def unstriped(offs):
    return offs[:16].T.reshape(-1).astype(np.int64)


def pack_weight(w):
    k, n = w.shape
    w = f64(np.asarray(w, np.float32).astype(ml_dtypes.bfloat16)).reshape(k // 32, 32, n)
    amax = np.abs(w).max(1)
    byte = np.clip(np.where(amax > 0, np.frexp(amax)[1] - 1 + 127 - 7, 1), 1, 254)
    scaled = (w * np.exp2(127.0 - byte)[:, None, :]).reshape(k, n).astype(np.float32)
    words = np.ascontiguousarray(scaled.reshape(k // 512, 128, 4, n).transpose(0, 1, 3, 2)).astype(ml_dtypes.float8_e4m3fn).view(np.uint8)
    return words, np.ascontiguousarray(byte.astype(np.uint8).reshape(k // 512, 16, n))


def unpack_weight(words, scales):
    g, p, n, _ = words.shape
    vals = np.ascontiguousarray(words).view(ml_dtypes.float8_e4m3fn).astype(np.float64) * np.repeat(np.exp2(scales.astype(np.float64) - 127.0), 8, axis=1)[..., None]
    return vals.transpose(0, 1, 3, 2).reshape(g * 512, n)


def relu(v):
    return np.maximum(v, 0.0)


K, T, H, N = 1024, 512, 512, 256


def setup_inputs():
    n = np.random.standard_normal
    s = mx_kscale(K)[:, None]
    u = mx_kscale(H)
    packed_xT = pack_weight(n((K, T)) * s)
    return {
        "x_words": packed_xT[0],
        "x_scales": packed_xT[1],
        "w1": (n((K, H)) / np.sqrt(K) / s * u).astype(np.float32),
        "w2": (n((H, N)) / np.sqrt(2 * H) / u[:, None]).astype(np.float32),
        "w3": (n((H, N)) / np.sqrt(2 * H) / u[:, None]).astype(np.float32),
        "pos1": striped(np.random.permutation(T)),
        "pos2": striped(np.random.permutation(T)),
    }


def reference(x_words, x_scales, w1, w2, w3, pos1, pos2):
    xq = unpack_weight(x_words, x_scales)
    h = relu(mxq(f64(w1), 0, "e4m3").T @ xq)
    z = (h[:, unstriped(pos1)] + h[:, unstriped(pos2)]) / 2
    return mxq(f64(w2), 0, "e4m3").T @ mxq(h, 0, "e4m3") + mxq(f64(w3), 0, "e4m3").T @ mxq(z, 0, "e4m3")

@@ -1,0 +1,193 @@
+from contextlib import ExitStack
+
+import concourse.mybir as mybir
+
+K, T, H, N = 1024, 512, 512, 256
+FLOPS = 2 * K * H * T + 2 * 2 * H * N * T
+
+F32 = mybir.dt.float32
+BF16 = mybir.dt.bfloat16
+I32 = mybir.dt.int32
+U32 = mybir.dt.uint32
+U16 = mybir.dt.uint16
+U8 = mybir.dt.uint8
+FP8X4 = mybir.dt.float8_e4m3fn_x4
+ACT = mybir.ActivationFunctionType
+ADD = mybir.AluOpType.add
+
+P = 128
+PACK = 4
+PASSES = K // (P * PACK)
+HEAD = 384
+TAIL = T - HEAD
+VECTOR_SHARE = 80
+
+
+def tile_picked_wsagecat_mean_l_kernel(
+    tc, x_words, x_scales, w1, w2, w3, pos1, pos2, out
+):
+    nc = tc.nc
+
+    def quantize(codes, scales, values):
+        nc.vector.quantize_mx(out=codes.bitcast(FP8X4), scales=scales, in_=values)
+
+    def matmul(acc, w_codes, w_scales, a_codes, a_scales, start, stop):
+        nc.tensor.matmul_mx(
+            out=acc,
+            lhsT=w_codes.bitcast(FP8X4),
+            lhsT_scale=w_scales,
+            rhs=a_codes.bitcast(FP8X4),
+            rhs_scale=a_scales,
+            start=start,
+            stop=stop,
+        )
+
+    with ExitStack() as ctx:
+        lists = ctx.enter_context(tc.tile_pool(name="lists", bufs=1))
+        sb = ctx.enter_context(tc.tile_pool(name="sb", bufs=1))
+        psum = ctx.enter_context(tc.psum_pool(name="psum", bufs=1))
+
+        x_planes = sb.tile([P, T], U8, name="x_planes", align_bytes=64)
+        nc.vector.memset(x_planes[:].bitcast(I32), 0)
+        w1_raw = []
+        for g in range(PASSES):
+            raw = sb.tile([P, PACK, H], F32, name="w1_raw%d" % g, tag="w1_raw%d" % g)
+            nc.sync.dma_start(
+                out=raw[:], in_=w1[g * 512 : (g + 1) * 512, :].rearrange("(p j) c -> p j c", j=PACK)
+            )
+            w1_raw.append(raw)
+            if g == 0:
+                for q in range(4):
+                    nc.sync.dma_start(
+                        out=x_planes[32 * q : 32 * q + 4 * PASSES, :].bitcast(I32),
+                        in_=x_scales[:, 4 * q : 4 * q + 4, :].bitcast(I32),
+                    )
+        x_codes = []
+        for g in range(PASSES):
+            codes = sb.tile([P, T], U32, name="x_codes%d" % g, align_bytes=64)
+            nc.sync.dma_start(
+                out=codes[:].bitcast(I32), in_=x_words[g].rearrange("p c r -> p (c r)").bitcast(I32)
+            )
+            x_codes.append(codes)
+        offsets = []
+        for d, pos in enumerate((pos1, pos2)):
+            offs = lists.tile([P, T // 16], U16, name="offsets%d" % d)
+            nc.sync.dma_start(offs[:], pos)
+            offsets.append(offs)
+
+        dealt = sb.tile([P, PACK, PASSES, P, PACK], BF16, name="w1_dealt", align_bytes=64)
+        flat = dealt[:].rearrange("p t g m j -> p (t g m j)")
+        w1_codes = sb.tile([P, PASSES * H], U32, name="w1_codes", align_bytes=64)
+        w1_scales = sb.tile([P, PASSES * H], U8, name="w1_scales", align_bytes=64)
+        for g in range(PASSES):
+            src = w1_raw[g][:].rearrange("p j (m t) -> p m j t", t=PACK)
+            dst = dealt[:, :, g].rearrange("p t m j -> p m j t")
+            if g == 0:
+                nc.vector.tensor_copy(out=dst, in_=src)
+            else:
+                nc.vector.tensor_copy(out=dst[:, :VECTOR_SHARE], in_=src[:, :VECTOR_SHARE])
+                nc.scalar.copy(out=dst[:, VECTOR_SHARE:], in_=src[:, VECTOR_SHARE:])
+            a, b = g * P, (g + 1) * P
+            quantize(w1_codes[:, a:b], w1_scales[:, a:b], flat[:, PACK * a : PACK * b])
+        for a, b in ((256, 512), (512, 1024)):
+            quantize(w1_codes[:, a:b], w1_scales[:, a:b], flat[:, PACK * a : PACK * b])
+
+        w_out_raw = sb.tile([P, 2, PACK, N], F32, name="w_out_raw", tag="w1_raw0")
+        for d, w in enumerate((w2, w3)):
+            nc.sync.dma_start(out=w_out_raw[:, d], in_=w.rearrange("(p j) c -> p j c", j=PACK))
+
+        half_row = sb.tile([P, PACK * T], F32, name="half_h")
+        for t in range(PACK):
+            acc = psum.tile([P, T], F32, name="h_acc%d" % t)
+            for g in range(PASSES):
+                cols = slice((t * PASSES + g) * P, (t * PASSES + g + 1) * P)
+                matmul(
+                    acc[:], w1_codes[:, cols], w1_scales[:, cols],
+                    x_codes[g][:], x_planes[4 * g :, :], g == 0, g == PASSES - 1,
+                )
+            nc.scalar.activation(out=half_row[:, t * T : (t + 1) * T], in_=acc[:], func=ACT.Relu, scale=0.5)
+
+        def gather(first, width, picked):
+            for t in range(PACK):
+                for d in range(2):
+                    nc.vector.tensor_copy(
+                        picked[d][:, t, :],
+                        half_row[:, t * T : (t + 1) * T].indirect(offsets[d][:, first // 16 : (first + width) // 16]),
+                    )
+
+        def mean(width, picked, name, tag):
+            z = sb.tile([P, width, PACK], BF16, name=name, tag=tag, align_bytes=64)
+            nc.vector.tensor_tensor(
+                z[:].rearrange("p (c i) t -> p c t i", i=4),
+                picked[0][:].rearrange("p t (c i) -> p c t i", i=4),
+                picked[1][:].rearrange("p t (c i) -> p c t i", i=4),
+                ADD,
+            )
+            return z[:].rearrange("p c t -> p (c t)")
+
+        picked_head = [sb.tile([P, PACK, HEAD], F32, name="picked_head%d" % d) for d in range(2)]
+        gather(0, HEAD, picked_head)
+
+        hw_bf = sb.tile([P, (T + 2 * N) * PACK], BF16, name="hw_bf", tag="reuse0", align_bytes=64)
+        nc.scalar.activation(
+            out=hw_bf[:, : T * PACK].rearrange("p (c i t) -> p c t i", i=4, t=PACK),
+            in_=half_row[:].rearrange("p (t c i) -> p c t i", t=PACK, i=4),
+            func=ACT.Copy,
+            scale=2.0,
+        )
+        for d in range(2):
+            first = (T + d * N) * PACK
+            nc.scalar.copy(
+                out=hw_bf[:, first : first + N * PACK].rearrange("p (c i j) -> p c j i", i=4, j=PACK),
+                in_=w_out_raw[:, d].rearrange("p j (c i) -> p c j i", i=4),
+            )
+
+        z_head = mean(HEAD, picked_head, "z_head", "reuse1")
+        hw_codes = sb.tile([P, T + 2 * N], U32, name="hw_codes", align_bytes=64)
+        hw_scales = sb.tile([P, T + 2 * N], U8, name="hw_scales", align_bytes=64)
+        quantize(hw_codes[:], hw_scales[:], hw_bf[:])
+        h_codes, h_scales = hw_codes[:, :T], hw_scales[:, :T]
+        w_codes, w_scales = hw_codes[:, T:], hw_scales[:, T:]
+        zh_codes = sb.tile([P, HEAD], U32, name="zh_codes", align_bytes=64)
+        zh_scales = sb.tile([P, HEAD], U8, name="zh_scales", align_bytes=64)
+        for a, b in ((0, 256), (256, HEAD)):
+            quantize(zh_codes[:, a:b], zh_scales[:, a:b], z_head[:, PACK * a : PACK * b])
+
+        picked_tail = [
+            sb.tile([P, PACK, TAIL], F32, name="picked_tail%d" % d, tag="reuse%d" % d, align_bytes=64)
+            for d in range(2)
+        ]
+        gather(HEAD, TAIL, picked_tail)
+
+        tail_acc = []
+        for m in range(N // P):
+            w2_cols = slice(m * P, (m + 1) * P)
+            w3_cols = slice(N + m * P, N + (m + 1) * P)
+            acc = psum.tile([P, HEAD], F32, name="head_acc%d" % m)
+            for a, b in ((0, 256), (256, HEAD)):
+                matmul(acc[:, a:b], w_codes[:, w2_cols], w_scales[:, w2_cols],
+                       h_codes[:, a:b], h_scales[:, a:b], True, False)
+                matmul(acc[:, a:b], w_codes[:, w3_cols], w_scales[:, w3_cols],
+                       zh_codes[:, a:b], zh_scales[:, a:b], False, True)
+            res = sb.tile([P, HEAD], F32, name="head_out%d" % m)
+            nc.scalar.copy(out=res[:], in_=acc[:])
+            nc.sync.dma_start(out=out[m * P : (m + 1) * P, :HEAD], in_=res[:])
+        for m in range(N // P):
+            w2_cols = slice(m * P, (m + 1) * P)
+            acc = psum.tile([P, TAIL], F32, name="tail_acc%d" % m)
+            matmul(acc[:], w_codes[:, w2_cols], w_scales[:, w2_cols],
+                   h_codes[:, HEAD:], h_scales[:, HEAD:], True, False)
+            tail_acc.append(acc)
+
+        z_tail = mean(TAIL, picked_tail, "z_tail", "z_tail")
+        zt_codes = sb.tile([P, TAIL], U32, name="zt_codes", align_bytes=64)
+        zt_scales = sb.tile([P, TAIL], U8, name="zt_scales", align_bytes=64)
+        quantize(zt_codes[:], zt_scales[:], z_tail)
+        res = sb.tile([P, N // P, TAIL], F32, name="tail_out")
+        for m in range(N // P):
+            w3_cols = slice(N + m * P, N + (m + 1) * P)
+            matmul(tail_acc[m][:], w_codes[:, w3_cols], w_scales[:, w3_cols],
+                   zt_codes[:], zt_scales[:], False, True)
+        nc.scalar.copy(out=res[:, 0, :], in_=tail_acc[0][:])
+        nc.vector.tensor_copy(out=res[:, 1, :], in_=tail_acc[1][:])
+        nc.sync.dma_start(out=out[:, HEAD:].rearrange("(m p) v -> p m v", p=P), in_=res[:])

@@ -1,6 +1,7 @@
 from contextlib import ExitStack
 
 import concourse.mybir as mybir
+from concourse.masks import make_identity
 
 K, T, H, N = 1024, 512, 512, 256
 FLOPS = 2 * K * H * T + 2 * 2 * H * N * T
@@ -18,9 +19,9 @@ ADD = mybir.AluOpType.add
 P = 128
 PACK = 4
 PASSES = K // (P * PACK)
-HEAD = 384
-TAIL = T - HEAD
+CHUNKS = ((0, 256), (256, 128), (384, 128))
 VECTOR_SHARE = 80
+W1_PIECES = ((0, 0, 4), (1, 0, 2), (1, 2, 4))
 
 
 def tile_picked_wsagecat_mean_l_kernel(
@@ -50,13 +51,13 @@ def tile_picked_wsagecat_mean_l_kernel(
         x_planes = sb.tile([P, T], U8, name="x_planes", align_bytes=64)
         nc.vector.memset(x_planes[:].bitcast(I32), 0)
         w1_raw = []
-        for g in range(PASSES):
-            raw = sb.tile([P, PACK, H], F32, name="w1_raw%d" % g, tag="w1_raw%d" % g)
+        for n, (g, j0, j1) in enumerate(W1_PIECES):
+            raw = sb.tile([P, j1 - j0, H], F32, name="w1_raw%d" % n, tag="w1_raw%d" % n)
             nc.sync.dma_start(
-                out=raw[:], in_=w1[g * 512 : (g + 1) * 512, :].rearrange("(p j) c -> p j c", j=PACK)
+                out=raw[:], in_=w1[g * 512 : (g + 1) * 512, :].rearrange("(p j) c -> p j c", j=PACK)[:, j0:j1]
             )
             w1_raw.append(raw)
-            if g == 0:
+            if n == 0:
                 for q in range(4):
                     nc.sync.dma_start(
                         out=x_planes[32 * q : 32 * q + 4 * PASSES, :].bitcast(I32),
@@ -79,16 +80,17 @@ def tile_picked_wsagecat_mean_l_kernel(
         flat = dealt[:].rearrange("p t g m j -> p (t g m j)")
         w1_codes = sb.tile([P, PASSES * H], U32, name="w1_codes", align_bytes=64)
         w1_scales = sb.tile([P, PASSES * H], U8, name="w1_scales", align_bytes=64)
-        for g in range(PASSES):
-            src = w1_raw[g][:].rearrange("p j (m t) -> p m j t", t=PACK)
-            dst = dealt[:, :, g].rearrange("p t m j -> p m j t")
+        for n, (g, j0, j1) in enumerate(W1_PIECES):
+            src = w1_raw[n][:].rearrange("p j (m t) -> p m j t", t=PACK)
+            dst = dealt[:, :, g, :, j0:j1].rearrange("p t m j -> p m j t")
             if g == 0:
                 nc.vector.tensor_copy(out=dst, in_=src)
             else:
                 nc.vector.tensor_copy(out=dst[:, :VECTOR_SHARE], in_=src[:, :VECTOR_SHARE])
                 nc.scalar.copy(out=dst[:, VECTOR_SHARE:], in_=src[:, VECTOR_SHARE:])
-            a, b = g * P, (g + 1) * P
-            quantize(w1_codes[:, a:b], w1_scales[:, a:b], flat[:, PACK * a : PACK * b])
+            if j1 == PACK:
+                a, b = g * P, (g + 1) * P
+                quantize(w1_codes[:, a:b], w1_scales[:, a:b], flat[:, PACK * a : PACK * b])
         for a, b in ((256, 512), (512, 1024)):
             quantize(w1_codes[:, a:b], w1_scales[:, a:b], flat[:, PACK * a : PACK * b])
 
@@ -97,36 +99,73 @@ def tile_picked_wsagecat_mean_l_kernel(
             nc.sync.dma_start(out=w_out_raw[:, d], in_=w.rearrange("(p j) c -> p j c", j=PACK))
 
         half_row = sb.tile([P, PACK * T], F32, name="half_h")
-        for t in range(PACK):
-            acc = psum.tile([P, T], F32, name="h_acc%d" % t)
+        pieces = [(0, 0, T // 2, "bank0"), (0, T // 2, T, "bank4")]
+        pieces = pieces + [(t, 0, T, "bank%d" % t) for t in range(1, PACK)]
+        for t, a, b, bank in pieces:
+            acc = psum.tile([P, b - a], F32, name="h_acc", tag=bank)
             for g in range(PASSES):
                 cols = slice((t * PASSES + g) * P, (t * PASSES + g + 1) * P)
                 matmul(
                     acc[:], w1_codes[:, cols], w1_scales[:, cols],
-                    x_codes[g][:], x_planes[4 * g :, :], g == 0, g == PASSES - 1,
+                    x_codes[g][:, a:b], x_planes[4 * g :, a:b], g == 0, g == PASSES - 1,
                 )
-            nc.scalar.activation(out=half_row[:, t * T : (t + 1) * T], in_=acc[:], func=ACT.Relu, scale=0.5)
+            nc.scalar.activation(out=half_row[:, t * T + a : t * T + b], in_=acc[:], func=ACT.Relu, scale=0.5)
 
-        def gather(first, width, picked):
+        identity = sb.tile([P, P], F32, name="identity")
+        make_identity(nc, identity[:])
+
+        def gather(chunk, tags):
+            first, width = CHUNKS[chunk]
+            picked = [
+                sb.tile([P, PACK, width], F32, name="picked%d_%d" % (chunk, d), tag=tags[d], align_bytes=64)
+                for d in range(2)
+            ]
+
+            def one(t, d):
+                nc.vector.tensor_copy(
+                    picked[d][:, t, :],
+                    half_row[:, t * T : (t + 1) * T].indirect(offsets[d][:, first // 16 : (first + width) // 16]),
+                )
+
+            return picked, one
+
+        def sum_turned(picked, block, bank):
+            acc = psum.tile([P, PACK, P], F32, name="turned", tag=bank)
             for t in range(PACK):
                 for d in range(2):
-                    nc.vector.tensor_copy(
-                        picked[d][:, t, :],
-                        half_row[:, t * T : (t + 1) * T].indirect(offsets[d][:, first // 16 : (first + width) // 16]),
+                    nc.tensor.matmul(
+                        acc[:, t, :], picked[d][:, t, block * P : (block + 1) * P], identity[:],
+                        start=d == 0, stop=d == 1, is_transpose=True,
                     )
+            return acc
 
-        def mean(width, picked, name, tag):
-            z = sb.tile([P, width, PACK], BF16, name=name, tag=tag, align_bytes=64)
-            nc.vector.tensor_tensor(
-                z[:].rearrange("p (c i) t -> p c t i", i=4),
-                picked[0][:].rearrange("p t (c i) -> p c t i", i=4),
-                picked[1][:].rearrange("p t (c i) -> p c t i", i=4),
-                ADD,
+        def turn_back(turned, z, tag, bank):
+            blocks = len(turned)
+            rounded = sb.tile([P, blocks, 2, P, 2], BF16, name="rounded", tag=tag)
+            for b in range(blocks):
+                nc.scalar.copy(out=rounded[:, b], in_=turned[b][:].rearrange("v (u e) p -> v u p e", e=2))
+            words = rounded[:].rearrange("v b u p e -> v (b u p e)").bitcast(F32)
+            back = psum.tile([P, blocks, 2, P], F32, name="back", tag=bank)
+            for b in range(blocks):
+                for u in range(2):
+                    nc.tensor.transpose(back[:, b, u, :], words[:, (2 * b + u) * P : (2 * b + u + 1) * P], identity[:])
+            nc.scalar.copy(
+                out=z[:].bitcast(F32).rearrange("p (b v u) -> p b v u", b=blocks, u=2),
+                in_=back[:].rearrange("p b u v -> p b v u"),
             )
-            return z[:].rearrange("p c t -> p (c t)")
 
-        picked_head = [sb.tile([P, PACK, HEAD], F32, name="picked_head%d" % d) for d in range(2)]
-        gather(0, HEAD, picked_head)
+        def quantised(values, width, name):
+            codes = sb.tile([P, width], U32, name=name + "_codes", align_bytes=64)
+            scales = sb.tile([P, width], U8, name=name + "_scales", align_bytes=64)
+            quantize(codes[:], scales[:], values)
+            return codes, scales
+
+        picked0, one0 = gather(0, ("p00", "p01"))
+        picked1, one1 = gather(1, ("p10", "p11"))
+        for one in (one0, one1):
+            for t in range(PACK):
+                for d in range(2):
+                    one(t, d)
 
         hw_bf = sb.tile([P, (T + 2 * N) * PACK], BF16, name="hw_bf", tag="reuse0", align_bytes=64)
         nc.scalar.activation(
@@ -141,53 +180,59 @@ def tile_picked_wsagecat_mean_l_kernel(
                 out=hw_bf[:, first : first + N * PACK].rearrange("p (c i j) -> p c j i", i=4, j=PACK),
                 in_=w_out_raw[:, d].rearrange("p j (c i) -> p c j i", i=4),
             )
+        turned0 = [sum_turned(picked0, b, "bank%d" % b) for b in range(2)]
+        turned1 = [sum_turned(picked1, 0, "bank2")]
+        hw_codes, hw_scales = quantised(hw_bf[:], T + 2 * N, "hw")
 
-        z_head = mean(HEAD, picked_head, "z_head", "reuse1")
-        hw_codes = sb.tile([P, T + 2 * N], U32, name="hw_codes", align_bytes=64)
-        hw_scales = sb.tile([P, T + 2 * N], U8, name="hw_scales", align_bytes=64)
-        quantize(hw_codes[:], hw_scales[:], hw_bf[:])
-        h_codes, h_scales = hw_codes[:, :T], hw_scales[:, :T]
-        w_codes, w_scales = hw_codes[:, T:], hw_scales[:, T:]
-        zh_codes = sb.tile([P, HEAD], U32, name="zh_codes", align_bytes=64)
-        zh_scales = sb.tile([P, HEAD], U8, name="zh_scales", align_bytes=64)
-        for a, b in ((0, 256), (256, HEAD)):
-            quantize(zh_codes[:, a:b], zh_scales[:, a:b], z_head[:, PACK * a : PACK * b])
+        z0 = sb.tile([P, 256 * PACK], BF16, name="z0", tag="reuse1", align_bytes=64)
+        turn_back(turned0, z0, "w1_raw0", "bank3")
+        z1 = sb.tile([P, 128 * PACK], BF16, name="z1", tag="reuse2", align_bytes=64)
+        turn_back(turned1, z1, "w1_raw0", "bank4")
 
-        picked_tail = [
-            sb.tile([P, PACK, TAIL], F32, name="picked_tail%d" % d, tag="reuse%d" % d, align_bytes=64)
-            for d in range(2)
-        ]
-        gather(HEAD, TAIL, picked_tail)
+        def h_pass(acc, m, chunk):
+            first, width = CHUNKS[chunk]
+            w2_cols = slice(T + m * P, T + (m + 1) * P)
+            matmul(acc, hw_codes[:, w2_cols], hw_scales[:, w2_cols],
+                   hw_codes[:, first : first + width], hw_scales[:, first : first + width], True, False)
 
-        tail_acc = []
-        for m in range(N // P):
-            w2_cols = slice(m * P, (m + 1) * P)
-            w3_cols = slice(N + m * P, N + (m + 1) * P)
-            acc = psum.tile([P, HEAD], F32, name="head_acc%d" % m)
-            for a, b in ((0, 256), (256, HEAD)):
-                matmul(acc[:, a:b], w_codes[:, w2_cols], w_scales[:, w2_cols],
-                       h_codes[:, a:b], h_scales[:, a:b], True, False)
-                matmul(acc[:, a:b], w_codes[:, w3_cols], w_scales[:, w3_cols],
-                       zh_codes[:, a:b], zh_scales[:, a:b], False, True)
-            res = sb.tile([P, HEAD], F32, name="head_out%d" % m)
+        def z_pass(acc, m, z_codes, z_scales):
+            w3_cols = slice(T + N + m * P, T + N + (m + 1) * P)
+            matmul(acc, hw_codes[:, w3_cols], hw_scales[:, w3_cols], z_codes[:], z_scales[:], False, True)
+
+        def finish(chunk, z, bank):
+            first, width = CHUNKS[chunk]
+            z_codes, z_scales = quantised(z[:], width, "z%d" % chunk)
+            acc = psum.tile([P, N // P, width], F32, name="out_acc", tag=bank)
+            for m in range(N // P):
+                h_pass(acc[:, m, :], m, chunk)
+                z_pass(acc[:, m, :], m, z_codes, z_scales)
+            res = sb.tile([P, N // P, width], F32, name="res%d" % chunk)
             nc.scalar.copy(out=res[:], in_=acc[:])
-            nc.sync.dma_start(out=out[m * P : (m + 1) * P, :HEAD], in_=res[:])
-        for m in range(N // P):
-            w2_cols = slice(m * P, (m + 1) * P)
-            acc = psum.tile([P, TAIL], F32, name="tail_acc%d" % m)
-            matmul(acc[:], w_codes[:, w2_cols], w_scales[:, w2_cols],
-                   h_codes[:, HEAD:], h_scales[:, HEAD:], True, False)
-            tail_acc.append(acc)
+            nc.sync.dma_start(out=out[:, first : first + width].rearrange("(m p) v -> p m v", p=P), in_=res[:])
 
-        z_tail = mean(TAIL, picked_tail, "z_tail", "z_tail")
-        zt_codes = sb.tile([P, TAIL], U32, name="zt_codes", align_bytes=64)
-        zt_scales = sb.tile([P, TAIL], U8, name="zt_scales", align_bytes=64)
-        quantize(zt_codes[:], zt_scales[:], z_tail)
-        res = sb.tile([P, N // P, TAIL], F32, name="tail_out")
+        first, width = CHUNKS[2]
+        tail_acc = [psum.tile([P, width], F32, name="tail_acc%d" % m) for m in range(N // P)]
         for m in range(N // P):
-            w3_cols = slice(N + m * P, N + (m + 1) * P)
-            matmul(tail_acc[m][:], w_codes[:, w3_cols], w_scales[:, w3_cols],
-                   zt_codes[:], zt_scales[:], False, True)
-        nc.scalar.copy(out=res[:, 0, :], in_=tail_acc[0][:])
-        nc.vector.tensor_copy(out=res[:, 1, :], in_=tail_acc[1][:])
-        nc.sync.dma_start(out=out[:, HEAD:].rearrange("(m p) v -> p m v", p=P), in_=res[:])
+            h_pass(tail_acc[m][:], m, 2)
+        finish(0, z0, "bank5")
+        picked2, one2 = gather(2, ("reuse0", "reuse1"))
+        for d in range(2):
+            for t in range(PACK):
+                one2(t, d)
+        finish(1, z1, "bank0")
+
+        z2 = sb.tile([P, width * PACK], BF16, name="z2", tag="reuse2", align_bytes=64)
+        nc.vector.tensor_tensor(
+            z2[:].rearrange("p (c i t) -> p c t i", i=4, t=PACK),
+            picked2[0][:].rearrange("p t (c i) -> p c t i", i=4),
+            picked2[1][:].rearrange("p t (c i) -> p c t i", i=4),
+            ADD,
+        )
+        z_codes, z_scales = quantised(z2[:], width, "z2")
+        for m in range(N // P):
+            z_pass(tail_acc[m][:], m, z_codes, z_scales)
+        res = [sb.tile([P, width], F32, name="res2_%d" % m) for m in range(N // P)]
+        nc.scalar.copy(out=res[0][:], in_=tail_acc[0][:])
+        nc.scalar.dma_start(out=out[:P, first:], in_=res[0][:])
+        nc.vector.tensor_copy(out=res[1][:], in_=tail_acc[1][:])
+        nc.sync.dma_start(out=out[P:, first:], in_=res[1][:])

@@ -20,8 +20,6 @@ P = 128
 PACK = 4
 PASSES = K // (P * PACK)
 CHUNKS = ((0, 256), (256, 128), (384, 128))
-VECTOR_SHARE = 80
-W1_PIECES = ((0, 0, 4), (1, 0, 2), (1, 2, 4))
 
 
 def tile_picked_wsagecat_mean_l_kernel(
@@ -51,13 +49,13 @@ def tile_picked_wsagecat_mean_l_kernel(
         x_planes = sb.tile([P, T], U8, name="x_planes", align_bytes=64)
         nc.vector.memset(x_planes[:].bitcast(I32), 0)
         w1_raw = []
-        for n, (g, j0, j1) in enumerate(W1_PIECES):
-            raw = sb.tile([P, j1 - j0, H], F32, name="w1_raw%d" % n, tag="w1_raw%d" % n)
+        for g in range(PASSES):
+            raw = sb.tile([P, PACK, H], F32, name="w1_raw%d" % g, tag="w1_raw%d" % g)
             nc.sync.dma_start(
-                out=raw[:], in_=w1[g * 512 : (g + 1) * 512, :].rearrange("(p j) c -> p j c", j=PACK)[:, j0:j1]
+                out=raw[:], in_=w1[g * 512 : (g + 1) * 512, :].rearrange("(p j) c -> p j c", j=PACK)
             )
             w1_raw.append(raw)
-            if n == 0:
+            if g == 0:
                 for q in range(4):
                     nc.sync.dma_start(
                         out=x_planes[32 * q : 32 * q + 4 * PASSES, :].bitcast(I32),
@@ -76,29 +74,34 @@ def tile_picked_wsagecat_mean_l_kernel(
             nc.sync.dma_start(offs[:], pos)
             offsets.append(offs)
 
-        dealt = sb.tile([P, PACK, PASSES, P, PACK], BF16, name="w1_dealt", align_bytes=64)
-        flat = dealt[:].rearrange("p t g m j -> p (t g m j)")
+        dealt = [sb.tile([P, 2, PASSES, P, PACK], BF16, name="w1_dealt%d" % u, align_bytes=64) for u in range(2)]
+        flat = [tile[:].rearrange("p e g m j -> p (e g m j)") for tile in dealt]
         w1_codes = sb.tile([P, PASSES * H], U32, name="w1_codes", align_bytes=64)
         w1_scales = sb.tile([P, PASSES * H], U8, name="w1_scales", align_bytes=64)
-        for n, (g, j0, j1) in enumerate(W1_PIECES):
-            src = w1_raw[n][:].rearrange("p j (m t) -> p m j t", t=PACK)
-            dst = dealt[:, :, g, :, j0:j1].rearrange("p t m j -> p m j t")
-            if g == 0:
-                nc.vector.tensor_copy(out=dst, in_=src)
-            else:
-                nc.vector.tensor_copy(out=dst[:, :VECTOR_SHARE], in_=src[:, :VECTOR_SHARE])
-                nc.scalar.copy(out=dst[:, VECTOR_SHARE:], in_=src[:, VECTOR_SHARE:])
-            if j1 == PACK:
-                a, b = g * P, (g + 1) * P
-                quantize(w1_codes[:, a:b], w1_scales[:, a:b], flat[:, PACK * a : PACK * b])
-        for a, b in ((256, 512), (512, 1024)):
-            quantize(w1_codes[:, a:b], w1_scales[:, a:b], flat[:, PACK * a : PACK * b])
+        for g in range(PASSES):
+            src = w1_raw[g][:].rearrange("p j (m u e) -> p u m j e", u=2, e=2)
+            nc.vector.tensor_copy(out=dealt[0][:, :, g].rearrange("p e m j -> p m j e"), in_=src[:, 0])
+            nc.scalar.copy(out=dealt[1][:, :, g].rearrange("p e m j -> p m j e"), in_=src[:, 1])
+            a, b = g * P, (g + 1) * P
+            quantize(w1_codes[:, a:b], w1_scales[:, a:b], flat[0][:, PACK * a : PACK * b])
+        quantize(w1_codes[:, 256:512], w1_scales[:, 256:512], flat[0][:, 1024:])
+        quantize(w1_codes[:, 512:], w1_scales[:, 512:], flat[1])
 
         w_out_raw = sb.tile([P, 2, PACK, N], F32, name="w_out_raw", tag="w1_raw0")
         for d, w in enumerate((w2, w3)):
             nc.sync.dma_start(out=w_out_raw[:, d], in_=w.rearrange("(p j) c -> p j c", j=PACK))
 
         half_row = sb.tile([P, PACK * T], F32, name="half_h")
+        hw_bf = sb.tile([P, (T + 2 * N) * PACK], BF16, name="hw_bf", tag="reuse0", align_bytes=64)
+
+        def round_w_out(piece):
+            d, half = divmod(piece, 2)
+            first = (T + piece * P) * PACK
+            nc.scalar.copy(
+                out=hw_bf[:, first : first + P * PACK].rearrange("p (c i j) -> p c j i", i=2, j=PACK),
+                in_=w_out_raw[:, d, :, half * P : (half + 1) * P].rearrange("p j (c i) -> p c j i", i=2),
+            )
+
         pieces = [(0, 0, T // 2, "bank0"), (0, T // 2, T, "bank4")]
         pieces = pieces + [(t, 0, T, "bank%d" % t) for t in range(1, PACK)]
         for t, a, b, bank in pieces:
@@ -110,34 +113,28 @@ def tile_picked_wsagecat_mean_l_kernel(
                     x_codes[g][:, a:b], x_planes[4 * g :, a:b], g == 0, g == PASSES - 1,
                 )
             nc.scalar.activation(out=half_row[:, t * T + a : t * T + b], in_=acc[:], func=ACT.Relu, scale=0.5)
+            if b == T:
+                round_w_out(t)
 
         identity = sb.tile([P, P], F32, name="identity")
         make_identity(nc, identity[:])
 
-        def gather(chunk, tags):
+        def gather(chunk, t, d, dst):
             first, width = CHUNKS[chunk]
-            picked = [
-                sb.tile([P, PACK, width], F32, name="picked%d_%d" % (chunk, d), tag=tags[d], align_bytes=64)
-                for d in range(2)
-            ]
+            nc.vector.tensor_copy(
+                dst, half_row[:, t * T : (t + 1) * T].indirect(offsets[d][:, first // 16 : (first + width) // 16])
+            )
 
-            def one(t, d):
-                nc.vector.tensor_copy(
-                    picked[d][:, t, :],
-                    half_row[:, t * T : (t + 1) * T].indirect(offsets[d][:, first // 16 : (first + width) // 16]),
-                )
-
-            return picked, one
-
-        def sum_turned(picked, block, bank):
-            acc = psum.tile([P, PACK, P], F32, name="turned", tag=bank)
+        def sum_turned(picked, banks):
+            turned = [psum.tile([P, PACK, P], F32, name="turned", tag=bank) for bank in banks]
             for t in range(PACK):
-                for d in range(2):
-                    nc.tensor.matmul(
-                        acc[:, t, :], picked[d][:, t, block * P : (block + 1) * P], identity[:],
-                        start=d == 0, stop=d == 1, is_transpose=True,
-                    )
-            return acc
+                for block, acc in enumerate(turned):
+                    for d in range(2):
+                        nc.tensor.matmul(
+                            acc[:, t, :], picked[t][d][:, block * P : (block + 1) * P], identity[:],
+                            start=d == 0, stop=d == 1, is_transpose=True,
+                        )
+            return turned
 
         def turn_back(turned, z, tag, bank):
             blocks = len(turned)
@@ -160,28 +157,27 @@ def tile_picked_wsagecat_mean_l_kernel(
             quantize(codes[:], scales[:], values)
             return codes, scales
 
-        picked0, one0 = gather(0, ("p00", "p01"))
-        picked1, one1 = gather(1, ("p10", "p11"))
-        for one in (one0, one1):
-            for t in range(PACK):
-                for d in range(2):
-                    one(t, d)
+        picked0 = [
+            [sb.tile([P, 256], F32, name="picked0", tag="picked%d_%d" % (t, d)) for d in range(2)]
+            for t in range(PACK)
+        ]
+        for t in range(PACK):
+            for d in range(2):
+                gather(0, t, d, picked0[t][d][:])
 
-        hw_bf = sb.tile([P, (T + 2 * N) * PACK], BF16, name="hw_bf", tag="reuse0", align_bytes=64)
         nc.scalar.activation(
-            out=hw_bf[:, : T * PACK].rearrange("p (c i t) -> p c t i", i=4, t=PACK),
-            in_=half_row[:].rearrange("p (t c i) -> p c t i", t=PACK, i=4),
+            out=hw_bf[:, : T * PACK].rearrange("p (c i t) -> p c t i", i=2, t=PACK),
+            in_=half_row[:].rearrange("p (t c i) -> p c t i", t=PACK, i=2),
             func=ACT.Copy,
             scale=2.0,
         )
-        for d in range(2):
-            first = (T + d * N) * PACK
-            nc.scalar.copy(
-                out=hw_bf[:, first : first + N * PACK].rearrange("p (c i j) -> p c j i", i=4, j=PACK),
-                in_=w_out_raw[:, d].rearrange("p j (c i) -> p c j i", i=4),
-            )
-        turned0 = [sum_turned(picked0, b, "bank%d" % b) for b in range(2)]
-        turned1 = [sum_turned(picked1, 0, "bank2")]
+        turned0 = sum_turned(picked0, ("bank0", "bank1"))
+        tiles1 = [sb.tile([P, PACK, 128], F32, name="picked1", tag="picked2_%d" % d) for d in range(2)]
+        picked1 = [[tiles1[d][:, t, :] for d in range(2)] for t in range(PACK)]
+        for t in range(PACK):
+            for d in range(2):
+                gather(1, t, d, picked1[t][d])
+        turned1 = sum_turned(picked1, ("bank2",))
         hw_codes, hw_scales = quantised(hw_bf[:], T + 2 * N, "hw")
 
         z0 = sb.tile([P, 256 * PACK], BF16, name="z0", tag="reuse1", align_bytes=64)
@@ -215,17 +211,19 @@ def tile_picked_wsagecat_mean_l_kernel(
         for m in range(N // P):
             h_pass(tail_acc[m][:], m, 2)
         finish(0, z0, "bank5")
-        picked2, one2 = gather(2, ("reuse0", "reuse1"))
+        picked2 = [
+            sb.tile([P, PACK, width], F32, name="picked2", tag="reuse%d" % d, align_bytes=64) for d in range(2)
+        ]
         for d in range(2):
             for t in range(PACK):
-                one2(t, d)
+                gather(2, t, d, picked2[d][:, t, :])
         finish(1, z1, "bank0")
 
         z2 = sb.tile([P, width * PACK], BF16, name="z2", tag="reuse2", align_bytes=64)
         nc.vector.tensor_tensor(
-            z2[:].rearrange("p (c i t) -> p c t i", i=4, t=PACK),
-            picked2[0][:].rearrange("p t (c i) -> p c t i", i=4),
-            picked2[1][:].rearrange("p t (c i) -> p c t i", i=4),
+            z2[:].rearrange("p (c i t) -> p c t i", i=2, t=PACK),
+            picked2[0][:].rearrange("p t (c i) -> p c t i", i=2),
+            picked2[1][:].rearrange("p t (c i) -> p c t i", i=2),
             ADD,
         )
         z_codes, z_scales = quantised(z2[:], width, "z2")

@@ -19,7 +19,9 @@ ADD = mybir.AluOpType.add
 P = 128
 PACK = 4
 PASSES = K // (P * PACK)
-CHUNKS = ((0, 256), (256, 128), (384, 128))
+LIST_ROWS = 16
+QUADRANT = 32
+RUNS = ((0, 2 * P), (2 * P, P), (3 * P, P))
 
 
 def tile_picked_wsagecat_mean_l_kernel(
@@ -46,19 +48,18 @@ def tile_picked_wsagecat_mean_l_kernel(
         sb = ctx.enter_context(tc.tile_pool(name="sb", bufs=1))
         psum = ctx.enter_context(tc.psum_pool(name="psum", bufs=1))
 
-        x_planes = sb.tile([P, T], U8, name="x_planes", align_bytes=64)
-        nc.vector.memset(x_planes[:].bitcast(I32), 0)
+        x_scale_tile = sb.tile([P, T], U8, name="x_scale_tile", align_bytes=64)
+        nc.vector.memset(x_scale_tile[:].bitcast(I32), 0)
         w1_raw = []
         for g in range(PASSES):
-            raw = sb.tile([P, PACK, H], F32, name="w1_raw%d" % g, tag="w1_raw%d" % g)
-            nc.sync.dma_start(
-                out=raw[:], in_=w1[g * 512 : (g + 1) * 512, :].rearrange("(p j) c -> p j c", j=PACK)
-            )
+            raw = sb.tile([P, PACK, H], F32, name="w1_raw", tag="stage%d" % g)
+            rows = w1[g * P * PACK : (g + 1) * P * PACK, :]
+            nc.sync.dma_start(out=raw[:], in_=rows.rearrange("(p j) c -> p j c", j=PACK))
             w1_raw.append(raw)
             if g == 0:
-                for q in range(4):
+                for q in range(P // QUADRANT):
                     nc.sync.dma_start(
-                        out=x_planes[32 * q : 32 * q + 4 * PASSES, :].bitcast(I32),
+                        out=x_scale_tile[QUADRANT * q : QUADRANT * q + 4 * PASSES, :].bitcast(I32),
                         in_=x_scales[:, 4 * q : 4 * q + 4, :].bitcast(I32),
                     )
         x_codes = []
@@ -70,60 +71,61 @@ def tile_picked_wsagecat_mean_l_kernel(
             x_codes.append(codes)
         offsets = []
         for d, pos in enumerate((pos1, pos2)):
-            offs = lists.tile([P, T // 16], U16, name="offsets%d" % d)
+            offs = lists.tile([P, T // LIST_ROWS], U16, name="offsets%d" % d)
             nc.sync.dma_start(offs[:], pos)
             offsets.append(offs)
 
         dealt = [sb.tile([P, 2, PASSES, P, PACK], BF16, name="w1_dealt%d" % u, align_bytes=64) for u in range(2)]
-        flat = [tile[:].rearrange("p e g m j -> p (e g m j)") for tile in dealt]
+        dealt_flat = [tile[:].rearrange("p e g m j -> p (e g m j)") for tile in dealt]
         w1_codes = sb.tile([P, PASSES * H], U32, name="w1_codes", align_bytes=64)
         w1_scales = sb.tile([P, PASSES * H], U8, name="w1_scales", align_bytes=64)
         for g in range(PASSES):
             src = w1_raw[g][:].rearrange("p j (m u e) -> p u m j e", u=2, e=2)
             nc.vector.tensor_copy(out=dealt[0][:, :, g].rearrange("p e m j -> p m j e"), in_=src[:, 0])
             nc.scalar.copy(out=dealt[1][:, :, g].rearrange("p e m j -> p m j e"), in_=src[:, 1])
-            a, b = g * P, (g + 1) * P
-            quantize(w1_codes[:, a:b], w1_scales[:, a:b], flat[0][:, PACK * a : PACK * b])
-        quantize(w1_codes[:, 256:512], w1_scales[:, 256:512], flat[0][:, 1024:])
-        quantize(w1_codes[:, 512:], w1_scales[:, 512:], flat[1])
+            cols = slice(g * P, (g + 1) * P)
+            quantize(w1_codes[:, cols], w1_scales[:, cols], dealt_flat[0][:, PACK * cols.start : PACK * cols.stop])
+        plane = PASSES * P
+        quantize(w1_codes[:, plane : 2 * plane], w1_scales[:, plane : 2 * plane], dealt_flat[0][:, PACK * plane :])
+        quantize(w1_codes[:, 2 * plane :], w1_scales[:, 2 * plane :], dealt_flat[1])
 
-        w_out_raw = sb.tile([P, 2, PACK, N], F32, name="w_out_raw", tag="w1_raw0")
+        w23_raw = sb.tile([P, 2 * PACK * N], F32, name="w23_raw", tag="stage0")
+        w23_rows = [w23_raw[:, d * PACK * N : (d + 1) * PACK * N] for d in range(2)]
         for d, w in enumerate((w2, w3)):
-            nc.sync.dma_start(out=w_out_raw[:, d], in_=w.rearrange("(p j) c -> p j c", j=PACK))
+            nc.sync.dma_start(out=w23_rows[d], in_=w.rearrange("(p j) c -> p (j c)", j=PACK))
 
-        half_row = sb.tile([P, PACK * T], F32, name="half_h")
-        hw_bf = sb.tile([P, (T + 2 * N) * PACK], BF16, name="hw_bf", tag="reuse0", align_bytes=64)
+        half_h = sb.tile([P, PACK * T], F32, name="half_h")
+        hw_bf = sb.tile([P, (T + 2 * N) * PACK], BF16, name="hw_bf", tag="quantised_hw", align_bytes=64)
 
-        def round_w_out(piece):
+        def round_w23(piece):
             d, half = divmod(piece, 2)
-            first = (T + piece * P) * PACK
+            start = (T + piece * P) * PACK
             nc.scalar.copy(
-                out=hw_bf[:, first : first + P * PACK].rearrange("p (c i j) -> p c j i", i=2, j=PACK),
-                in_=w_out_raw[:, d, :, half * P : (half + 1) * P].rearrange("p j (c i) -> p c j i", i=2),
+                out=hw_bf[:, start : start + P * PACK].rearrange("p (c i j) -> p c j i", i=2, j=PACK),
+                in_=w23_rows[d].rearrange("p (j h c i) -> p h c j i", j=PACK, h=2, i=2)[:, half],
             )
 
-        pieces = [(0, 0, T // 2, "bank0"), (0, T // 2, T, "bank4")]
-        pieces = pieces + [(t, 0, T, "bank%d" % t) for t in range(1, PACK)]
-        for t, a, b, bank in pieces:
+        groups = [(0, 0, T // 2, "bank0"), (0, T // 2, T, "bank4")]
+        groups = groups + [(t, 0, T, "bank%d" % t) for t in range(1, PACK)]
+        for t, a, b, bank in groups:
             acc = psum.tile([P, b - a], F32, name="h_acc", tag=bank)
             for g in range(PASSES):
-                cols = slice((t * PASSES + g) * P, (t * PASSES + g + 1) * P)
+                cols = slice(t * plane + g * P, t * plane + (g + 1) * P)
                 matmul(
                     acc[:], w1_codes[:, cols], w1_scales[:, cols],
-                    x_codes[g][:, a:b], x_planes[4 * g :, a:b], g == 0, g == PASSES - 1,
+                    x_codes[g][:, a:b], x_scale_tile[4 * g :, a:b], g == 0, g == PASSES - 1,
                 )
-            nc.scalar.activation(out=half_row[:, t * T + a : t * T + b], in_=acc[:], func=ACT.Relu, scale=0.5)
+            nc.scalar.activation(out=half_h[:, t * T + a : t * T + b], in_=acc[:], func=ACT.Relu, scale=0.5)
             if b == T:
-                round_w_out(t)
+                round_w23(t)
 
         identity = sb.tile([P, P], F32, name="identity")
         make_identity(nc, identity[:])
 
-        def gather(chunk, t, d, dst):
-            first, width = CHUNKS[chunk]
-            nc.vector.tensor_copy(
-                dst, half_row[:, t * T : (t + 1) * T].indirect(offsets[d][:, first // 16 : (first + width) // 16])
-            )
+        def gather(run, t, d, dst):
+            first, width = RUNS[run]
+            entries = offsets[d][:, first // LIST_ROWS : (first + width) // LIST_ROWS]
+            nc.vector.tensor_copy(dst, half_h[:, t * T : (t + 1) * T].indirect(entries))
 
         def sum_turned(picked, banks):
             turned = [psum.tile([P, PACK, P], F32, name="turned", tag=bank) for bank in banks]
@@ -136,20 +138,18 @@ def tile_picked_wsagecat_mean_l_kernel(
                         )
             return turned
 
-        def turn_back(turned, z, tag, bank):
-            blocks = len(turned)
-            rounded = sb.tile([P, blocks, 2, P, 2], BF16, name="rounded", tag=tag)
-            for b in range(blocks):
-                nc.scalar.copy(out=rounded[:, b], in_=turned[b][:].rearrange("v (u e) p -> v u p e", e=2))
-            words = rounded[:].rearrange("v b u p e -> v (b u p e)").bitcast(F32)
-            back = psum.tile([P, blocks, 2, P], F32, name="back", tag=bank)
-            for b in range(blocks):
+        def turn_back(turned, z, banks):
+            rounded = sb.tile([P, len(turned), 2, P, 2], BF16, name="rounded", tag="stage0")
+            for block, acc in enumerate(turned):
+                nc.scalar.copy(out=rounded[:, block], in_=acc[:].rearrange("v (u e) p -> v u p e", e=2))
+            pairs = rounded[:].rearrange("v b u p e -> v (b u p e)").bitcast(F32)
+            for block, bank in enumerate(banks):
+                back = psum.tile([P, 2, P], F32, name="back", tag=bank)
                 for u in range(2):
-                    nc.tensor.transpose(back[:, b, u, :], words[:, (2 * b + u) * P : (2 * b + u + 1) * P], identity[:])
-            nc.scalar.copy(
-                out=z[:].bitcast(F32).rearrange("p (b v u) -> p b v u", b=blocks, u=2),
-                in_=back[:].rearrange("p b u v -> p b v u"),
-            )
+                    start = (2 * block + u) * P
+                    nc.tensor.transpose(back[:, u, :], pairs[:, start : start + P], identity[:])
+                z_pairs = z[:, block * P * PACK : (block + 1) * P * PACK].bitcast(F32)
+                nc.scalar.copy(out=z_pairs.rearrange("p (v u) -> p v u", u=2), in_=back[:].rearrange("p u v -> p v u"))
 
         def quantised(values, width, name):
             codes = sb.tile([P, width], U32, name=name + "_codes", align_bytes=64)
@@ -158,7 +158,7 @@ def tile_picked_wsagecat_mean_l_kernel(
             return codes, scales
 
         picked0 = [
-            [sb.tile([P, 256], F32, name="picked0", tag="picked%d_%d" % (t, d)) for d in range(2)]
+            [sb.tile([P, RUNS[0][1]], F32, name="picked0", tag="picked%d_%d" % (t, d)) for d in range(2)]
             for t in range(PACK)
         ]
         for t in range(PACK):
@@ -167,12 +167,13 @@ def tile_picked_wsagecat_mean_l_kernel(
 
         nc.scalar.activation(
             out=hw_bf[:, : T * PACK].rearrange("p (c i t) -> p c t i", i=2, t=PACK),
-            in_=half_row[:].rearrange("p (t c i) -> p c t i", t=PACK, i=2),
+            in_=half_h[:].rearrange("p (t c i) -> p c t i", t=PACK, i=2),
             func=ACT.Copy,
             scale=2.0,
         )
         turned0 = sum_turned(picked0, ("bank0", "bank1"))
-        tiles1 = [sb.tile([P, PACK, 128], F32, name="picked1", tag="picked2_%d" % d) for d in range(2)]
+
+        tiles1 = [sb.tile([P, PACK, RUNS[1][1]], F32, name="picked1", tag="picked2_%d" % d) for d in range(2)]
         picked1 = [[tiles1[d][:, t, :] for d in range(2)] for t in range(PACK)]
         for t in range(PACK):
             for d in range(2):
@@ -180,57 +181,61 @@ def tile_picked_wsagecat_mean_l_kernel(
         turned1 = sum_turned(picked1, ("bank2",))
         hw_codes, hw_scales = quantised(hw_bf[:], T + 2 * N, "hw")
 
-        z0 = sb.tile([P, 256 * PACK], BF16, name="z0", tag="reuse1", align_bytes=64)
-        turn_back(turned0, z0, "w1_raw0", "bank3")
-        z1 = sb.tile([P, 128 * PACK], BF16, name="z1", tag="reuse2", align_bytes=64)
-        turn_back(turned1, z1, "w1_raw0", "bank4")
+        z0 = sb.tile([P, RUNS[0][1] * PACK], BF16, name="z0", tag="quantised_z0", align_bytes=64)
+        turn_back(turned0, z0, ("bank3", "bank5"))
+        z1 = sb.tile([P, RUNS[1][1] * PACK], BF16, name="z1", tag="quantised_z1", align_bytes=64)
+        turn_back(turned1, z1, ("bank4",))
 
-        def h_pass(acc, m, chunk):
-            first, width = CHUNKS[chunk]
+        def h_pass(acc, m, run, opens):
+            first, width = RUNS[run]
             w2_cols = slice(T + m * P, T + (m + 1) * P)
-            matmul(acc, hw_codes[:, w2_cols], hw_scales[:, w2_cols],
-                   hw_codes[:, first : first + width], hw_scales[:, first : first + width], True, False)
+            matmul(
+                acc, hw_codes[:, w2_cols], hw_scales[:, w2_cols],
+                hw_codes[:, first : first + width], hw_scales[:, first : first + width], opens, not opens,
+            )
 
-        def z_pass(acc, m, z_codes, z_scales):
+        def z_pass(acc, m, z_codes, z_scales, opens):
             w3_cols = slice(T + N + m * P, T + N + (m + 1) * P)
-            matmul(acc, hw_codes[:, w3_cols], hw_scales[:, w3_cols], z_codes[:], z_scales[:], False, True)
+            matmul(acc, hw_codes[:, w3_cols], hw_scales[:, w3_cols], z_codes[:], z_scales[:], opens, not opens)
 
-        def finish(chunk, z, bank):
-            first, width = CHUNKS[chunk]
-            z_codes, z_scales = quantised(z[:], width, "z%d" % chunk)
+        def finish(run, z, bank):
+            first, width = RUNS[run]
+            z_codes, z_scales = quantised(z[:], width, "z%d" % run)
             acc = psum.tile([P, N // P, width], F32, name="out_acc", tag=bank)
             for m in range(N // P):
-                h_pass(acc[:, m, :], m, chunk)
-                z_pass(acc[:, m, :], m, z_codes, z_scales)
-            res = sb.tile([P, N // P, width], F32, name="res%d" % chunk)
+                z_pass(acc[:, m, :], m, z_codes, z_scales, True)
+                h_pass(acc[:, m, :], m, run, False)
+            res = sb.tile([P, N // P, width], F32, name="res%d" % run)
             nc.scalar.copy(out=res[:], in_=acc[:])
             nc.sync.dma_start(out=out[:, first : first + width].rearrange("(m p) v -> p m v", p=P), in_=res[:])
 
-        first, width = CHUNKS[2]
-        tail_acc = [psum.tile([P, width], F32, name="tail_acc%d" % m) for m in range(N // P)]
+        last_first, last_width = RUNS[2]
+        last_acc = [psum.tile([P, last_width], F32, name="last_acc", tag=bank) for bank in ("bank3", "bank5")]
         for m in range(N // P):
-            h_pass(tail_acc[m][:], m, 2)
-        finish(0, z0, "bank5")
+            h_pass(last_acc[m][:], m, 2, True)
+        finish(0, z0, "bank0")
+
         picked2 = [
-            sb.tile([P, PACK, width], F32, name="picked2", tag="reuse%d" % d, align_bytes=64) for d in range(2)
+            sb.tile([P, PACK, last_width], F32, name="picked2", tag=tag, align_bytes=64)
+            for tag in ("quantised_hw", "quantised_z0")
         ]
         for d in range(2):
             for t in range(PACK):
                 gather(2, t, d, picked2[d][:, t, :])
-        finish(1, z1, "bank0")
+        finish(1, z1, "bank1")
 
-        z2 = sb.tile([P, width * PACK], BF16, name="z2", tag="reuse2", align_bytes=64)
+        z2 = sb.tile([P, last_width * PACK], BF16, name="z2", tag="quantised_z1", align_bytes=64)
         nc.vector.tensor_tensor(
             z2[:].rearrange("p (c i t) -> p c t i", i=2, t=PACK),
             picked2[0][:].rearrange("p t (c i) -> p c t i", i=2),
             picked2[1][:].rearrange("p t (c i) -> p c t i", i=2),
             ADD,
         )
-        z_codes, z_scales = quantised(z2[:], width, "z2")
+        z2_codes, z2_scales = quantised(z2[:], last_width, "z2")
         for m in range(N // P):
-            z_pass(tail_acc[m][:], m, z_codes, z_scales)
-        res = [sb.tile([P, width], F32, name="res2_%d" % m) for m in range(N // P)]
-        nc.scalar.copy(out=res[0][:], in_=tail_acc[0][:])
-        nc.scalar.dma_start(out=out[:P, first:], in_=res[0][:])
-        nc.vector.tensor_copy(out=res[1][:], in_=tail_acc[1][:])
-        nc.sync.dma_start(out=out[P:, first:], in_=res[1][:])
+            z_pass(last_acc[m][:], m, z2_codes, z2_scales, False)
+        last_res = [sb.tile([P, last_width], F32, name="last_res%d" % m) for m in range(N // P)]
+        nc.scalar.copy(out=last_res[0][:], in_=last_acc[0][:])
+        nc.scalar.dma_start(out=out[:P, last_first:], in_=last_res[0][:])
+        nc.vector.tensor_copy(out=last_res[1][:], in_=last_acc[1][:])
+        nc.sync.dma_start(out=out[P:, last_first:], in_=last_res[1][:])

from contextlib import ExitStack

import concourse.mybir as mybir
from concourse.masks import make_identity

K, T, H, N = 1024, 512, 512, 256
FLOPS = 2 * K * H * T + 2 * 2 * H * N * T

F32 = mybir.dt.float32
BF16 = mybir.dt.bfloat16
I32 = mybir.dt.int32
U32 = mybir.dt.uint32
U16 = mybir.dt.uint16
U8 = mybir.dt.uint8
FP8X4 = mybir.dt.float8_e4m3fn_x4
ACT = mybir.ActivationFunctionType
ADD = mybir.AluOpType.add

P = 128
PACK = 4
PASSES = K // (P * PACK)
LIST_ROWS = 16
QUADRANT = 32
RUNS = ((0, 2 * P), (2 * P, P), (3 * P, P))


def tile_picked_wsagecat_mean_l_kernel(
    tc, x_words, x_scales, w1, w2, w3, pos1, pos2, out
):
    nc = tc.nc

    def quantize(codes, scales, values):
        nc.vector.quantize_mx(out=codes.bitcast(FP8X4), scales=scales, in_=values)

    def matmul(acc, w_codes, w_scales, a_codes, a_scales, start, stop):
        nc.tensor.matmul_mx(
            out=acc,
            lhsT=w_codes.bitcast(FP8X4),
            lhsT_scale=w_scales,
            rhs=a_codes.bitcast(FP8X4),
            rhs_scale=a_scales,
            start=start,
            stop=stop,
        )

    with ExitStack() as ctx:
        lists = ctx.enter_context(tc.tile_pool(name="lists", bufs=1))
        sb = ctx.enter_context(tc.tile_pool(name="sb", bufs=1))
        psum = ctx.enter_context(tc.psum_pool(name="psum", bufs=1))

        x_scale_tile = sb.tile([P, T], U8, name="x_scale_tile", align_bytes=64)
        nc.vector.memset(x_scale_tile[:].bitcast(I32), 0)
        w1_raw = []
        for g in range(PASSES):
            raw = sb.tile([P, PACK, H], F32, name="w1_raw", tag="stage%d" % g)
            rows = w1[g * P * PACK : (g + 1) * P * PACK, :]
            nc.sync.dma_start(out=raw[:], in_=rows.rearrange("(p j) c -> p j c", j=PACK))
            w1_raw.append(raw)
            if g == 0:
                for q in range(P // QUADRANT):
                    nc.sync.dma_start(
                        out=x_scale_tile[QUADRANT * q : QUADRANT * q + 4 * PASSES, :].bitcast(I32),
                        in_=x_scales[:, 4 * q : 4 * q + 4, :].bitcast(I32),
                    )
        x_codes = []
        for g in range(PASSES):
            codes = sb.tile([P, T], U32, name="x_codes%d" % g, align_bytes=64)
            nc.sync.dma_start(
                out=codes[:].bitcast(I32), in_=x_words[g].rearrange("p c r -> p (c r)").bitcast(I32)
            )
            x_codes.append(codes)
        offsets = []
        for d, pos in enumerate((pos1, pos2)):
            offs = lists.tile([P, T // LIST_ROWS], U16, name="offsets%d" % d)
            nc.sync.dma_start(offs[:], pos)
            offsets.append(offs)

        dealt = [sb.tile([P, 2, PASSES, P, PACK], BF16, name="w1_dealt%d" % u, align_bytes=64) for u in range(2)]
        dealt_flat = [tile[:].rearrange("p e g m j -> p (e g m j)") for tile in dealt]
        w1_codes = sb.tile([P, PASSES * H], U32, name="w1_codes", align_bytes=64)
        w1_scales = sb.tile([P, PASSES * H], U8, name="w1_scales", align_bytes=64)
        for g in range(PASSES):
            src = w1_raw[g][:].rearrange("p j (m u e) -> p u m j e", u=2, e=2)
            nc.vector.tensor_copy(out=dealt[0][:, :, g].rearrange("p e m j -> p m j e"), in_=src[:, 0])
            nc.scalar.copy(out=dealt[1][:, :, g].rearrange("p e m j -> p m j e"), in_=src[:, 1])
            cols = slice(g * P, (g + 1) * P)
            quantize(w1_codes[:, cols], w1_scales[:, cols], dealt_flat[0][:, PACK * cols.start : PACK * cols.stop])
        plane = PASSES * P
        quantize(w1_codes[:, plane : 2 * plane], w1_scales[:, plane : 2 * plane], dealt_flat[0][:, PACK * plane :])
        quantize(w1_codes[:, 2 * plane :], w1_scales[:, 2 * plane :], dealt_flat[1])

        w23_raw = sb.tile([P, 2 * PACK * N], F32, name="w23_raw", tag="stage0")
        w23_rows = [w23_raw[:, d * PACK * N : (d + 1) * PACK * N] for d in range(2)]
        for d, w in enumerate((w2, w3)):
            nc.sync.dma_start(out=w23_rows[d], in_=w.rearrange("(p j) c -> p (j c)", j=PACK))

        half_h = sb.tile([P, PACK * T], F32, name="half_h")
        hw_bf = sb.tile([P, (T + 2 * N) * PACK], BF16, name="hw_bf", tag="quantised_hw", align_bytes=64)

        def round_w23(piece):
            d, half = divmod(piece, 2)
            start = (T + piece * P) * PACK
            nc.scalar.copy(
                out=hw_bf[:, start : start + P * PACK].rearrange("p (c i j) -> p c j i", i=2, j=PACK),
                in_=w23_rows[d].rearrange("p (j h c i) -> p h c j i", j=PACK, h=2, i=2)[:, half],
            )

        groups = [(0, 0, T // 2, "bank0"), (0, T // 2, T, "bank4")]
        groups = groups + [(t, 0, T, "bank%d" % t) for t in range(1, PACK)]
        for t, a, b, bank in groups:
            acc = psum.tile([P, b - a], F32, name="h_acc", tag=bank)
            for g in range(PASSES):
                cols = slice(t * plane + g * P, t * plane + (g + 1) * P)
                matmul(
                    acc[:], w1_codes[:, cols], w1_scales[:, cols],
                    x_codes[g][:, a:b], x_scale_tile[4 * g :, a:b], g == 0, g == PASSES - 1,
                )
            nc.scalar.activation(out=half_h[:, t * T + a : t * T + b], in_=acc[:], func=ACT.Relu, scale=0.5)
            if b == T:
                round_w23(t)

        identity = sb.tile([P, P], F32, name="identity")
        make_identity(nc, identity[:])

        def gather(run, t, d, dst):
            first, width = RUNS[run]
            entries = offsets[d][:, first // LIST_ROWS : (first + width) // LIST_ROWS]
            nc.vector.tensor_copy(dst, half_h[:, t * T : (t + 1) * T].indirect(entries))

        def sum_turned(picked, banks):
            turned = [psum.tile([P, PACK, P], F32, name="turned", tag=bank) for bank in banks]
            for t in range(PACK):
                for block, acc in enumerate(turned):
                    for d in range(2):
                        nc.tensor.matmul(
                            acc[:, t, :], picked[t][d][:, block * P : (block + 1) * P], identity[:],
                            start=d == 0, stop=d == 1, is_transpose=True,
                        )
            return turned

        def turn_back(turned, z, banks):
            rounded = sb.tile([P, len(turned), 2, P, 2], BF16, name="rounded", tag="stage0")
            for block, acc in enumerate(turned):
                nc.scalar.copy(out=rounded[:, block], in_=acc[:].rearrange("v (u e) p -> v u p e", e=2))
            pairs = rounded[:].rearrange("v b u p e -> v (b u p e)").bitcast(F32)
            for block, bank in enumerate(banks):
                back = psum.tile([P, 2, P], F32, name="back", tag=bank)
                for u in range(2):
                    start = (2 * block + u) * P
                    nc.tensor.transpose(back[:, u, :], pairs[:, start : start + P], identity[:])
                z_pairs = z[:, block * P * PACK : (block + 1) * P * PACK].bitcast(F32)
                nc.scalar.copy(out=z_pairs.rearrange("p (v u) -> p v u", u=2), in_=back[:].rearrange("p u v -> p v u"))

        def quantised(values, width, name):
            codes = sb.tile([P, width], U32, name=name + "_codes", align_bytes=64)
            scales = sb.tile([P, width], U8, name=name + "_scales", align_bytes=64)
            quantize(codes[:], scales[:], values)
            return codes, scales

        picked0 = [
            [sb.tile([P, RUNS[0][1]], F32, name="picked0", tag="picked%d_%d" % (t, d)) for d in range(2)]
            for t in range(PACK)
        ]
        for t in range(PACK):
            for d in range(2):
                gather(0, t, d, picked0[t][d][:])

        nc.scalar.activation(
            out=hw_bf[:, : T * PACK].rearrange("p (c i t) -> p c t i", i=2, t=PACK),
            in_=half_h[:].rearrange("p (t c i) -> p c t i", t=PACK, i=2),
            func=ACT.Copy,
            scale=2.0,
        )
        turned0 = sum_turned(picked0, ("bank0", "bank1"))

        tiles1 = [sb.tile([P, PACK, RUNS[1][1]], F32, name="picked1", tag="picked2_%d" % d) for d in range(2)]
        picked1 = [[tiles1[d][:, t, :] for d in range(2)] for t in range(PACK)]
        for t in range(PACK):
            for d in range(2):
                gather(1, t, d, picked1[t][d])
        turned1 = sum_turned(picked1, ("bank2",))
        hw_codes, hw_scales = quantised(hw_bf[:], T + 2 * N, "hw")

        z0 = sb.tile([P, RUNS[0][1] * PACK], BF16, name="z0", tag="quantised_z0", align_bytes=64)
        turn_back(turned0, z0, ("bank3", "bank5"))
        z1 = sb.tile([P, RUNS[1][1] * PACK], BF16, name="z1", tag="quantised_z1", align_bytes=64)
        turn_back(turned1, z1, ("bank4",))

        def h_pass(acc, m, run, opens):
            first, width = RUNS[run]
            w2_cols = slice(T + m * P, T + (m + 1) * P)
            matmul(
                acc, hw_codes[:, w2_cols], hw_scales[:, w2_cols],
                hw_codes[:, first : first + width], hw_scales[:, first : first + width], opens, not opens,
            )

        def z_pass(acc, m, z_codes, z_scales, opens):
            w3_cols = slice(T + N + m * P, T + N + (m + 1) * P)
            matmul(acc, hw_codes[:, w3_cols], hw_scales[:, w3_cols], z_codes[:], z_scales[:], opens, not opens)

        def finish(run, z, bank):
            first, width = RUNS[run]
            z_codes, z_scales = quantised(z[:], width, "z%d" % run)
            acc = psum.tile([P, N // P, width], F32, name="out_acc", tag=bank)
            for m in range(N // P):
                z_pass(acc[:, m, :], m, z_codes, z_scales, True)
                h_pass(acc[:, m, :], m, run, False)
            res = sb.tile([P, N // P, width], F32, name="res%d" % run)
            nc.scalar.copy(out=res[:], in_=acc[:])
            nc.sync.dma_start(out=out[:, first : first + width].rearrange("(m p) v -> p m v", p=P), in_=res[:])

        last_first, last_width = RUNS[2]
        last_acc = [psum.tile([P, last_width], F32, name="last_acc", tag=bank) for bank in ("bank3", "bank5")]
        for m in range(N // P):
            h_pass(last_acc[m][:], m, 2, True)
        finish(0, z0, "bank0")

        picked2 = [
            sb.tile([P, PACK, last_width], F32, name="picked2", tag=tag, align_bytes=64)
            for tag in ("quantised_hw", "quantised_z0")
        ]
        for d in range(2):
            for t in range(PACK):
                gather(2, t, d, picked2[d][:, t, :])
        finish(1, z1, "bank1")

        z2 = sb.tile([P, last_width * PACK], BF16, name="z2", tag="quantised_z1", align_bytes=64)
        nc.vector.tensor_tensor(
            z2[:].rearrange("p (c i t) -> p c t i", i=2, t=PACK),
            picked2[0][:].rearrange("p t (c i) -> p c t i", i=2),
            picked2[1][:].rearrange("p t (c i) -> p c t i", i=2),
            ADD,
        )
        z2_codes, z2_scales = quantised(z2[:], last_width, "z2")
        for m in range(N // P):
            z_pass(last_acc[m][:], m, z2_codes, z2_scales, False)
        last_res = [sb.tile([P, last_width], F32, name="last_res%d" % m) for m in range(N // P)]
        nc.scalar.copy(out=last_res[0][:], in_=last_acc[0][:])
        nc.scalar.dma_start(out=out[:P, last_first:], in_=last_res[0][:])
        nc.vector.tensor_copy(out=last_res[1][:], in_=last_acc[1][:])
        nc.sync.dma_start(out=out[P:, last_first:], in_=last_res[1][:])
